import numpy as np
import ml_dtypes


def mxq(x, axis, fmt="e4m3"):
    dtype, down = {"e4m3": (ml_dtypes.float8_e4m3fn, 7), "e5m2": (ml_dtypes.float8_e5m2, 14)}[fmt]
    v = np.moveaxis(np.asarray(x, np.float32).astype(ml_dtypes.bfloat16).astype(np.float64), axis, -1)
    blocks = v.reshape(v.shape[:-1] + (-1, 32))
    amax = np.abs(blocks).max(-1, keepdims=True)
    byte = np.maximum(np.where(amax > 0, np.frexp(amax)[1] - 1 + 127, 0) - down, 1)
    scale = np.exp2(byte - 127.0)
    codes = (blocks / scale).astype(np.float32).astype(dtype).astype(np.float64)
    return np.moveaxis((codes * scale).reshape(v.shape), -1, axis)


WIDE = False


def mx_kscale(k):
    if not WIDE:
        return np.ones(k)
    levels = np.array([10, -10, 5, -5, 0])
    if k % 512:
        return np.exp2(np.random.permutation(np.resize(levels, k // 32))).repeat(32)
    a = np.empty((k // 512, 16))
    for p in range(k // 512):
        a[p, :8] = np.random.permutation(np.resize(levels, 8))
        for g in range(8):
            far = levels[np.abs(levels - a[p, g]) >= 10]
            a[p, g + 8] = far[np.random.randint(len(far))]
    return np.exp2(a.ravel()).repeat(32)


BF16 = ml_dtypes.bfloat16


def bf(x):
    return np.asarray(x, np.float32).astype(BF16)


def f64(x):
    return np.asarray(x).astype(np.float64)


E2M1 = np.array([0.0, 0.5, 1.0, 1.5, 2.0, 3.0, 4.0, 6.0, -0.0, -0.5, -1.0, -1.5, -2.0, -3.0, -4.0, -6.0])


def pack_weight(w, fmt):
    k, n = w.shape
    w = f64(bf(w)).reshape(k // 32, 32, n)
    amax = np.abs(w).max(1)
    if fmt == "e4m3":
        byte = np.frexp(amax)[1] - 1 + 127 - 7
    else:
        mant, ex = np.frexp(amax / 6.0)
        byte = np.where(mant > 0.5, ex, ex - 1) + 127
    byte = np.clip(np.where(amax > 0, byte, 1), 1, 254)
    scaled = (w * np.exp2(127.0 - byte)[:, None, :]).reshape(k, n).astype(np.float32)
    by_word = np.ascontiguousarray(scaled.reshape(k // 512, 128, 4, n).transpose(0, 1, 3, 2))
    if fmt == "e4m3":
        words = by_word.astype(ml_dtypes.float8_e4m3fn).view(np.uint8)
    else:
        c = by_word.astype(ml_dtypes.float4_e2m1fn).view(np.uint8) & 0xF
        words = c[..., 0::2] | (c[..., 1::2] << 4)
    return np.ascontiguousarray(words), np.ascontiguousarray(byte.astype(np.uint8).reshape(k // 512, 16, n))


def unpack_weight(words, scales, fmt):
    g, p, n, _ = words.shape
    if fmt == "e4m3":
        vals = np.ascontiguousarray(words).view(ml_dtypes.float8_e4m3fn).astype(np.float64)
    else:
        nib = np.empty((g, p, n, 4), np.uint8)
        nib[..., 0::2] = words & 0xF
        nib[..., 1::2] = words >> 4
        vals = E2M1[nib]
    vals = vals * np.repeat(np.exp2(scales.astype(np.float64) - 127.0), 8, axis=1)[..., None]
    return vals.transpose(0, 1, 3, 2).reshape(g * 512, n)

E4M3FN = np.array([(-1.0 if i & 128 else 1.0) * ((1.0 + (i & 7) / 8.0) * 2.0 ** (((i >> 3) & 15) - 7) if i & 120 else (i & 7) * 2.0 ** -9) for i in range(256)])


def e4m3fn_bytes(y):
    return np.clip(np.asarray(y, np.float64), -448.0, 448.0).astype(np.float32).astype(ml_dtypes.float8_e4m3fn).view(np.uint8)


def e4m3fn_values(b):
    return E4M3FN[b]


S, F, G, T, C = 1024, 1024, 1024, 512, 512


def smooth_modulus(re, im):
    return np.sqrt(re * re + im * im + 0.25)


def draw0():
    s, t = mx_kscale(S), mx_kscale(F)
    a_scale = 1.0 / np.sqrt(S)
    c_scale = 1.5 / np.sqrt(F)
    x = bf(np.random.standard_normal((S, C)) * s[:, None])
    ar_words, ar_scales = pack_weight((np.random.standard_normal((F, S)) * a_scale / s[None, :]).T, "e4m3")
    aim_words, aim_scales = pack_weight((np.random.standard_normal((F, S)) * a_scale / s[None, :]).T, "e4m3")
    g1 = bf((1.0 + 0.1 * np.random.standard_normal(F)) * t)
    cr_words, cr_scales = pack_weight((np.random.standard_normal((G, F)) * c_scale / t[None, :]).T, "e4m3")
    cim_words, cim_scales = pack_weight((np.random.standard_normal((G, F)) * c_scale / t[None, :]).T, "e4m3")
    phi_words, phi_scales = pack_weight((np.random.standard_normal((T, F)) * c_scale / t[None, :]).T, "e4m3")
    return {
        "x": x,
        "ar_words": ar_words,
        "ar_scales": ar_scales,
        "aim_words": aim_words,
        "aim_scales": aim_scales,
        "g1": g1,
        "cr_words": cr_words,
        "cr_scales": cr_scales,
        "cim_words": cim_words,
        "cim_scales": cim_scales,
        "phi_words": phi_words,
        "phi_scales": phi_scales,
    }


def core(x, ar_words, ar_scales, aim_words, aim_scales, g1, cr_words, cr_scales, cim_words, cim_scales, phi_words, phi_scales):
    xq = mxq(f64(x), 0, "e4m3")
    r1 = unpack_weight(ar_words, ar_scales, "e4m3").T @ xq
    i1 = unpack_weight(aim_words, aim_scales, "e4m3").T @ xq
    u1 = smooth_modulus(r1, i1)
    n1 = f64(g1)[:, None] * (u1 - np.mean(u1, axis=0, keepdims=True))
    nq = mxq(n1, 0, "e4m3")
    s1 = unpack_weight(phi_words, phi_scales, "e4m3").T @ nq
    r2 = unpack_weight(cr_words, cr_scales, "e4m3").T @ nq
    i2 = unpack_weight(cim_words, cim_scales, "e4m3").T @ nq
    u2 = smooth_modulus(r2, i2)
    return s1, u2


def setup_inputs():
    drawn = draw0()
    full = np.asarray(drawn['x']).astype(np.float64)
    scale = (np.abs(full).reshape(8, 128, 4, 128).max(axis=(1, 3)) / 448.0).astype(np.float32)
    given = {}
    for key, value in drawn.items():
        if key == 'x':
            given['x_bytes'] = e4m3fn_bytes(full / np.repeat(np.repeat(scale.astype(np.float64), 128, axis=0), 128, axis=1))
            given['x_scale'] = scale
        else:
            given[key] = value
    return given


def reference(x_bytes, x_scale, ar_words, ar_scales, aim_words, aim_scales, g1, cr_words, cr_scales, cim_words, cim_scales, phi_words, phi_scales):
    return core(e4m3fn_values(x_bytes) * np.repeat(np.repeat(x_scale.astype(np.float64), 128, axis=0), 128, axis=1), ar_words, ar_scales, aim_words, aim_scales, g1, cr_words, cr_scales, cim_words, cim_scales, phi_words, phi_scales)

from contextlib import ExitStack

import concourse.mybir as mybir
from concourse.masks import make_identity

S, F, G, T, C = 1024, 1024, 1024, 512, 512
FLOPS = 2 * C * (2 * F * S + (T + 2 * G) * F)

F32 = mybir.dt.float32
BF16 = mybir.dt.bfloat16
I32 = mybir.dt.int32
U32 = mybir.dt.uint32
U8 = mybir.dt.uint8
FP8 = mybir.dt.float8_e4m3fn
FP8X4 = mybir.dt.float8_e4m3fn_x4
ALU = mybir.AluOpType
ACT = mybir.ActivationFunctionType

P = 128
PASSES = 2
CT = 128
N_CT = C // CT
HALF = 512
PAIR = 256

V_SQUARES = ((1, 0), (1, 2),)
S_SCALES = ((0, 0),)
ORDER = """
gm.0 xi.1.0 xi.0.0 xi.1.1 xs.1.0 gm.1 xs.1.1 xi.0.1 xs.0.0 xq.1 gc.1 xs.0.1
xi.2.0 xq.0 xs.2.0 gc.0 m1.1.0.0 sq.1.0.0 m1.1.0.1 sq.1.0.1 xi.3.0 m1.0.0.1 m1.0.0.0 xi.3.1
xi.2.1 sq.0.0.1 xs.3.1 m1.0.1.0 sq.0.0.0 xs.3.0 m1.1.1.0 xs.2.1 m1.0.1.1 sq.0.1.0 xq.3 xq.2
sq.1.1.0 ad.1.0 ad.0.0 sq.0.1.1 m1.1.1.1 sq.1.1.1 ad.0.1 ad.1.1 m1.2.1.0 m1.2.1.1 rt.0 m1.2.0.1
m1.2.0.0 m1.3.0.1 m1.3.0.0 rt.1 sq.2.1.0 sq.2.1.1 mn.0 ct.0 m1.3.1.0 mn.1 ct.1 sq.2.0.1
tr.0 m1.3.1.1 to.0 sq.2.0.0 sq.3.0.1 sq.3.1.0 ad.2.1 sq.3.0.0 tr.1 ad.2.0 sq.3.1.1 to.1
rt.2 mn.2 nq.0 nq.1 ad.3.0 ad.3.1 ct.2 m2.0.2.1 rt.3 m2.0.2.0 m2.0.1.1 sq2.0.2.0
mn.3 ct.3 m2.0.0.1 m2.0.3.0 tr.2 m2.0.1.0 sq2.0.1.1 m2.0.3.1 sq2.0.2.1 sq2.0.3.0 sq2.0.1.0 to.2
ad2.0.2 sq2.0.0.1 tr.3 rt2.0.2 m2.0.0.0 sq2.0.3.1 sq2.0.0.0 mp.0.1 ad2.0.1 to.3 nq.2 nq.3
rt2.0.1 ad2.0.3 mp.0.0 ad2.0.0 m2.1.3.1 rt2.0.3 rt2.0.0 sq2.1.3.1 cp.0.1 m2.1.3.0 sq2.1.3.0 m2.1.2.1
m2.1.0.1 m2.1.1.1 sq2.1.1.1 cp.0.0 m2.1.0.0 vc2.1.2 vc2.1.0 sq2.1.2.1 m2.1.2.0 sq2.1.0.0 sq2.1.0.1 m2.1.1.0
ad2.1.3 sq2.1.2.0 mp.1.0 sq2.1.1.0 rt2.1.3 ad2.1.0 ad2.1.2 mp.1.1 rt2.1.0 rt2.1.2 ad2.1.1 cp.1.1
cp.1.0 rt2.1.1
"""


def tile_learnedsecondorderscattering_d2p_kernel(
    tc, x_bytes, x_scale, ar_words, ar_scales, aim_words, aim_scales, g1,
    cr_words, cr_scales, cim_words, cim_scales, phi_words, phi_scales, s1_out, u2_out,
):
    nc = tc.nc
    with ExitStack() as ctx:
        keep = ctx.enter_context(tc.tile_pool(name="keep", bufs=1))
        work = ctx.enter_context(tc.tile_pool(name="work", bufs=5))
        mm = ctx.enter_context(tc.psum_pool(name="mm", bufs=7))
        tp = ctx.enter_context(tc.psum_pool(name="tp", bufs=1))
        ctx.enter_context(tc.manual_schedule())

        x_raw = keep.tile([P, PASSES, 4, C], U8, name="x_raw", align_bytes=64)
        scale_all = keep.tile([P, 32], F32, name="scale_all")
        scale_col = keep.tile([P, PASSES, N_CT], F32, name="scale_col")
        g_row = keep.tile([P, F], BF16, name="g_row")
        ones = keep.tile([P, P], BF16, name="ones")
        g_all = keep.tile([P, F], BF16, name="g_all")
        ident = keep.tile([P, P], F32, name="ident")
        warm = keep.tile([P, 1], F32, name="warm")

        def plane(name, width):
            return keep.tile([P, PASSES, width], U8, name=name, align_bytes=64)

        ar_s, aim_s = plane("ar_s", F), plane("aim_s", F)
        cr_s, cim_s, phi_s = plane("cr_s", G), plane("cim_s", G), plane("phi_s", T)

        def words_tiles(name, count):
            return [keep.tile([P, PASSES, HALF], U32, name="%s%d" % (name, h), align_bytes=64) for h in range(count)]

        ar_w, aim_w = words_tiles("ar_w", 2), words_tiles("aim_w", 2)
        cr_w, cim_w, phi_w = words_tiles("cr_w", 2), words_tiles("cim_w", 2), words_tiles("phi_w", 1)

        def load_scales(queue, dst, src, quads=(0, 1, 2, 3)):
            view = src.bitcast(I32).rearrange("g q n -> q g n")
            for q in quads:
                queue.dma_start(out=dst[32 * q : 32 * q + 4, :, :].bitcast(I32), in_=view[4 * q : 4 * q + 4, :, :])

        def load_words(queue, dst, src, h):
            view = src.rearrange("g p n t -> p g (n t)")[:, :, 4 * HALF * h : 4 * HALF * (h + 1)]
            queue.dma_start(out=dst[h][:].bitcast(I32), in_=view.bitcast(I32))

        nc.vector.memset(ar_s[:].bitcast(I32), 0)
        nc.vector.memset(aim_s[:].bitcast(I32), 0)
        nc.vector.memset(g_row[:].bitcast(I32), 0)
        nc.vector.memset(ones[:], 1.0)

        x_view = x_bytes.rearrange("(g p t) n -> g p t n", p=P, t=4)
        for g in range(PASSES):
            nc.sync.dma_start(out=x_raw[:, g, :, :], in_=x_view[g])
        nc.gpsimd.dma_start(out=scale_all[:], in_=x_scale.rearrange("a b -> (a b)").partition_broadcast(P))
        nc.gpsimd.dma_start(out=g_row[0:1, :], in_=g1.rearrange("(o f) -> o f", o=1))
        load_words(nc.sync, ar_w, ar_words, 0)
        load_scales(nc.scalar, ar_s, ar_scales)
        load_words(nc.sync, aim_w, aim_words, 0)
        load_scales(nc.sync, aim_s, aim_scales)
        load_words(nc.sync, ar_w, ar_words, 1)
        load_words(nc.sync, aim_w, aim_words, 1)
        nc.gpsimd.memset(cr_s[:].bitcast(I32), 0)
        nc.gpsimd.memset(cim_s[:].bitcast(I32), 0)
        nc.gpsimd.memset(phi_s[:].bitcast(I32), 0)
        load_words(nc.sync, cr_w, cr_words, 0)
        load_scales(nc.sync, cr_s, cr_scales)
        load_words(nc.sync, cim_w, cim_words, 0)
        load_scales(nc.sync, cim_s, cim_scales)
        load_words(nc.sync, cr_w, cr_words, 1)
        load_words(nc.sync, cim_w, cim_words, 1)
        load_words(nc.sync, phi_w, phi_words, 0)
        load_scales(nc.sync, phi_s, phi_scales)

        make_identity(nc, ident[:])
        nc.scalar.activation(out=warm[:], in_=ones[:, 0:1], func=ACT.Sqrt)
        for q in range(4):
            rows = slice(32 * q, 32 * q + 32)
            nc.vector.tensor_copy(
                out=scale_col[rows, :, :],
                in_=scale_all[rows, :].rearrange("p (g q b) -> p g q b", g=PASSES, q=4)[:, :, q, :],
            )

        xi, xv, xq, xs = {}, {}, {}, {}

        def x_interleave(i, g):
            if i not in xi:
                xi[i] = keep.tile([P, PASSES, CT, 4], U8, name="xi%d" % i, align_bytes=64)
            nc.vector.tensor_copy(out=xi[i][:, g, :, :], in_=x_raw[:, g, :, CT * i : CT * (i + 1)].rearrange("p t c -> p c t"))

        def x_scaled(i, g):
            if i not in xv:
                xv[i] = keep.tile([P, PASSES, 4 * CT], BF16, name="xv%d" % i, align_bytes=64)
            src = xi[i][:, g, :, :].rearrange("p c t -> p (c t)").bitcast(FP8)
            col = scale_col[:, g, i : i + 1]
            if (i, g) in S_SCALES:
                nc.scalar.activation(out=xv[i][:, g, :], in_=src, func=ACT.Copy, scale=col)
            else:
                nc.vector.tensor_scalar(out=xv[i][:, g, :], in0=src, scalar1=col, scalar2=None, op0=ALU.mult)

        def x_quantize(i):
            xq[i] = keep.tile([P, PASSES, CT], U32, name="xq%d" % i, align_bytes=64)
            xs[i] = keep.tile([P, PASSES, CT], U8, name="xs%d" % i, align_bytes=64)
            nc.vector.quantize_mx(
                out=xq[i][:].rearrange("p g c -> p (g c)").bitcast(FP8X4),
                scales=xs[i][:].rearrange("p g c -> p (g c)"),
                in_=xv[i][:].rearrange("p g c -> p (g c)"),
            )

        bank, sqa, sqb, u1, mean, n1, nt, ntb = {}, {}, {}, {}, {}, {}, {}, {}

        def gain_matmul(h):
            bank["g", h] = mm.tile([P, HALF], F32, name="acc")
            nc.tensor.matmul(bank["g", h][:], lhsT=ones[:], rhs=g_row[:, HALF * h : HALF * (h + 1)], start=True, stop=True)

        def gain_copy(h):
            nc.scalar.copy(out=g_all[:, HALF * h : HALF * (h + 1)], in_=bank["g", h][:])

        def first_bank(i, h, part):
            w, s = ((ar_w, ar_s), (aim_w, aim_s))[part]
            acc = mm.tile([P, HALF], F32, name="acc")
            bank[i, h, part] = acc
            for g in range(PASSES):
                nc.tensor.matmul_mx(
                    out=acc[:],
                    lhsT=xq[i][:, g, :].bitcast(FP8X4),
                    lhsT_scale=xs[i][:, g, :],
                    rhs=w[h][:, g, :].bitcast(FP8X4),
                    rhs_scale=s[:, g, HALF * h : HALF * (h + 1)],
                    start=(g == 0),
                    stop=(g == PASSES - 1),
                )

        def first_square(i, h, part):
            if i not in sqa:
                sqa[i] = work.tile([P, F], F32, name="sqa")
                sqb[i] = work.tile([P, F], F32, name="sqb")
            t = (sqa, sqb)[part][i]
            nc.scalar.activation(out=t[:, HALF * h : HALF * (h + 1)], in_=bank[i, h, part][:], func=ACT.Square)

        def first_add(i, h):
            cols = slice(HALF * h, HALF * (h + 1))
            nc.vector.tensor_tensor(out=sqa[i][:, cols], in0=sqa[i][:, cols], in1=sqb[i][:, cols], op=ALU.add)

        def first_sqrt(i):
            u1[i] = work.tile([P, F], F32, name="u1")
            mean[i] = [work.tile([P, 1], F32, name="total"), work.tile([P, 1], F32, name="mean")]
            nc.scalar.activation(out=u1[i][:], in_=sqa[i][:], func=ACT.Sqrt, bias=0.25, accum_out=mean[i][0][:])

        def first_mean(i):
            nc.gpsimd.tensor_scalar(
                out=mean[i][1][:], in0=mean[i][0][:], scalar1=1.0 / F, scalar2=0.0, op0=ALU.mult, op1=ALU.add
            )

        def centre(i):
            n1[i] = work.tile([P, F], BF16, name="n1", align_bytes=64)
            nc.vector.scalar_tensor_tensor(
                out=n1[i][:], in0=u1[i][:], scalar=mean[i][1][:], in1=g_all[:], op0=ALU.subtract, op1=ALU.mult
            )

        def turn(i):
            nt[i] = tp.tile([P, PASSES, 2, CT], F32, name="nt")
            words = n1[i][:].bitcast(F32)
            for g in range(PASSES):
                for u in range(2):
                    nc.tensor.transpose(nt[i][:, g, u, :], words[:, 256 * g + u : 256 * (g + 1) : 2], ident[:])

        def turn_out(i):
            ntb[i] = work.tile([P, PASSES, 4 * CT], BF16, name="ntb", align_bytes=64)
            nc.vector.tensor_copy(
                out=ntb[i][:].bitcast(F32).rearrange("p g (c u) -> p g c u", u=2),
                in_=nt[i][:].rearrange("p g u c -> p g c u"),
            )

        nq = [keep.tile([P, PASSES, PAIR], U32, name="nq%d" % k, align_bytes=64) for k in range(2)]
        ns = [keep.tile([P, PASSES, PAIR], U8, name="ns%d" % k, align_bytes=64) for k in range(2)]

        def n_quantize(i):
            cols = slice(CT * (i % 2), CT * (i % 2) + CT)
            for g in range(PASSES):
                nc.vector.quantize_mx(
                    out=nq[i // 2][:, g, cols].bitcast(FP8X4), scales=ns[i // 2][:, g, cols], in_=ntb[i][:, g, :]
                )

        bank2, sq2 = {}, {}

        def second_bank(k, j, part):
            w, s = ((cr_w, cr_s), (cim_w, cim_s), (phi_w, phi_s))[part]
            acc = mm.tile([P, 2, PAIR], F32, name="acc")
            bank2[k, j, part] = acc
            for r in range(2):
                m = 2 * j + r
                h, c0 = m // 4, P * (m % 4)
                for g in range(PASSES):
                    nc.tensor.matmul_mx(
                        out=acc[:, r, :],
                        lhsT=w[h][:, g, c0 : c0 + P].bitcast(FP8X4),
                        lhsT_scale=s[:, g, P * m : P * m + P],
                        rhs=nq[k][:, g, :].bitcast(FP8X4),
                        rhs_scale=ns[k][:, g, :],
                        start=(g == 0),
                        stop=(g == PASSES - 1),
                    )

        def second_copy(k, j):
            sq2[k, j, 1] = work.tile([P, 2, PAIR], F32, name="sq2_1")
            nc.vector.tensor_copy(out=sq2[k, j, 1][:], in_=bank2[k, j, 1][:])

        def second_square(k, j, part):
            if part == 1 and (k, j) in V_SQUARES:
                t = sq2[k, j, 1]
                nc.vector.tensor_tensor(out=t[:], in0=bank2[k, j, 1][:], in1=t[:], op=ALU.mult)
            else:
                t = work.tile([P, 2, PAIR], F32, name="sq2_%d" % part)
                sq2[k, j, part] = t
                nc.scalar.activation(out=t[:], in_=bank2[k, j, part][:], func=ACT.Square)

        def second_add(k, j):
            nc.vector.tensor_tensor(out=sq2[k, j, 0][:], in0=sq2[k, j, 0][:], in1=sq2[k, j, 1][:], op=ALU.add)

        u2_view = u2_out.rearrange("(m p) c -> p m c", p=P)
        s1_view = s1_out.rearrange("(m p) c -> p m c", p=P)

        def second_sqrt(k, j):
            t = work.tile([P, 2, PAIR], F32, name="u2")
            nc.scalar.activation(out=t[:], in_=sq2[k, j, 0][:], func=ACT.Sqrt, bias=0.25)
            nc.sync.dma_start(out=u2_view[:, 2 * j : 2 * j + 2, PAIR * k : PAIR * (k + 1)], in_=t[:])

        def coefficients(k, j):
            second_bank(k, j, 2)

        def coefficients_out(k, j):
            t = work.tile([P, 2, PAIR], F32, name="s1")
            nc.vector.tensor_copy(out=t[:], in_=bank2[k, j, 2][:])
            nc.sync.dma_start(out=s1_view[:, 2 * j : 2 * j + 2, PAIR * k : PAIR * (k + 1)], in_=t[:])

        steps = {
            "xi": x_interleave, "xs": x_scaled, "xq": x_quantize, "gm": gain_matmul, "gc": gain_copy,
            "m1": first_bank, "sq": first_square, "ad": first_add, "rt": first_sqrt, "mn": first_mean,
            "ct": centre, "tr": turn, "to": turn_out, "nq": n_quantize, "m2": second_bank, "vc2": second_copy,
            "sq2": second_square, "ad2": second_add, "rt2": second_sqrt, "mp": coefficients, "cp": coefficients_out,
        }
        for word in ORDER.split():
            parts = word.split(".")
            steps[parts[0]](*[int(v) for v in parts[1:]])
